import numpy as np
CORES = [7,15,23,31,39,47,55,63,71,79]
N = 10
def setup_inputs(rng):
    return {"x": rng.standard_normal((N, 128, 256), dtype=np.float32)}
def reference(x):
    s = np.maximum.accumulate(x, axis=0)
    return {"y": s.astype(x.dtype)}

@@ -1,0 +1,88 @@
+from concourse.bass import DstId, RemoteDMATransfer
+
+S = 4
+HELP = [5, 6, 2, 3]
+RANK_CORE = 7
+NCHIP = 10
+NPAIR = NCHIP // 2
+W = 32768 // S // 128
+ROWS = 128 // S
+MAX = 2
+
+SCRATCH = {
+    "xs": ("dram", [S, 128, W], "float32"),
+    "res": ("dram", [S, 128, W], "float32"),
+    "own": ("dram", [128, W], "float32"),
+    "mate": ("dram", [128, W], "float32"),
+    "pre": ("dram", [NPAIR - 1, 128, W], "float32"),
+}
+SEMAPHORES = ["ld", "st", "in1", "in2", "sent"]
+
+
+def _bits(lo, n):
+    return ((1 << n) - 1) << lo
+
+
+def _needs_mate(chip):
+    return chip % 2 == 1 or chip // 2 < NPAIR - 1
+
+
+def rank_program(g, core, T, topo):
+    chip, k_on_chip = topo.chip(core), core % 8
+    if chip >= NCHIP:
+        return
+    pair, par = chip // 2, chip % 2
+
+    def dst(c):
+        rid, pid, _se = topo.addr(c)
+        return DstId(rid=rid, pnc=pid)
+
+    e1 = 8 // S
+
+    if k_on_chip == RANK_CORE:
+        g.sync.dma_start(T.xs[:], T.x[:]).then_inc(T.sem.ld, 16)
+        if chip == 0:
+            g.scalar.dma_start(T.y[:], T.x[:]).then_inc(T.sem.st, 16)
+        g.wait_ge(T.sem.ld, 16)
+        tr = []
+        for s in range(S):
+            tr.append(RemoteDMATransfer(dst_ids=[dst(chip * 8 + HELP[s])], dma_engine_mask=_bits(8 + s * e1, e1),
+                                        remote_sem=T.sem.in1, src=T.xs[s], dst=T.own[:]))
+            if _needs_mate(chip ^ 1):
+                tr.append(RemoteDMATransfer(dst_ids=[dst((chip ^ 1) * 8 + HELP[s])], dma_engine_mask=_bits(s * e1, e1),
+                                            remote_sem=T.sem.in1, src=T.xs[s], dst=T.mate[:]))
+        g.remote_dma_fused(tr, local_sem=T.sem.sent)
+        if chip > 0:
+            g.sync.wait_ge(T.sem.in2, S * (8 if chip == 1 else 16))
+            g.sync.dma_start(T.y[:], T.res[:]).then_inc(T.sem.st, 16)
+        g.wait_ge(T.sem.sent, e1 * len(tr))
+        g.wait_ge(T.sem.st, 16)
+        return
+
+    if k_on_chip not in HELP:
+        return
+    s = HELP.index(k_on_chip)
+    rank_core = chip * 8 + RANK_CORE
+    sent = 0
+    g.wait_ge(T.sem.in1, e1 * (2 if _needs_mate(chip) else 1))
+
+    if pair < NPAIR - 1:
+        ids = [dst((2 * q + par) * 8 + k_on_chip) for q in range(pair + 1, NPAIR)]
+        outs = [T.pre[pair] for _q in range(pair + 1, NPAIR)]
+        if chip == 1:
+            ids.append(dst(rank_core))
+            outs.append(T.res[s])
+        g.remote_dma_fused([RemoteDMATransfer(dst_ids=ids, dma_engine_mask=0x00FF, remote_sem=T.sem.in2,
+                                              srcs=[T.own[:], T.mate[:]], dsts=outs, alu_op=MAX)],
+                           local_sem=T.sem.sent)
+        sent += 8
+
+    if pair > 0:
+        g.wait_ge(T.sem.in2, 8 * pair)
+        srcs = [T.pre[j] for j in range(pair)] + [T.own[:]] + ([T.mate[:]] if par else [])
+        g.remote_dma_fused([RemoteDMATransfer(dst_ids=[dst(rank_core)], dma_engine_mask=0xFFFF, remote_sem=T.sem.in2,
+                                              srcs=srcs, dsts=[T.res[s]], alu_op=MAX)],
+                           local_sem=T.sem.sent)
+        sent += 16
+
+    g.wait_ge(T.sem.sent, sent)

@@ -1,20 +1,21 @@
 from concourse.bass import DstId, RemoteDMATransfer
 
-S = 4
-HELP = [5, 6, 2, 3]
-RANK_CORE = 7
 NCHIP = 10
-NPAIR = NCHIP // 2
-W = 32768 // S // 128
-ROWS = 128 // S
+RANK_CORE = 7
+HELP = [2, 3]
+NH = len(HELP)
+SMALL = 2
+WB, WA = 24 // NH, 26 // NH
+ROWS_B = SMALL * 12
 MAX = 2
 
 SCRATCH = {
-    "xs": ("dram", [S, 128, W], "float32"),
-    "res": ("dram", [S, 128, W], "float32"),
-    "own": ("dram", [128, W], "float32"),
-    "mate": ("dram", [128, W], "float32"),
-    "pre": ("dram", [NPAIR - 1, 128, W], "float32"),
+    "xsB": ("dram", [SMALL * NH, 128, WB], "float32"),
+    "xsA": ("dram", [(NCHIP - SMALL) * NH, 128, WA], "float32"),
+    "resB": ("dram", [SMALL * NH, 128, WB], "float32"),
+    "resA": ("dram", [(NCHIP - SMALL) * NH, 128, WA], "float32"),
+    "gB": ("dram", [NCHIP, 128, WB], "float32"),
+    "gA": ("dram", [NCHIP, 128, WA], "float32"),
 }
 SEMAPHORES = ["ld", "st", "in1", "in2", "sent"]
 
@@ -23,66 +24,95 @@ def _bits(lo, n):
     return ((1 << n) - 1) << lo
 
 
-def _needs_mate(chip):
-    return chip % 2 == 1 or chip // 2 < NPAIR - 1
+def _pop(m):
+    return bin(m).count("1")
+
+
+def _plan1(j):
+    calls = []
+    for h in range(NH):
+        call, e = [], 0
+        for o in range(SMALL, NCHIP):
+            if o == j:
+                call.append((o, h, 0xFF00))
+            else:
+                call.append((o, h, _bits(e, 1)))
+                e += 1
+        calls.append(call)
+    units = [(o, h) for o in range(SMALL) for h in range(NH)]
+    off = [u for u in units if u[0] != j]
+    on = [u for u in units if u[0] == j]
+    call = [(o, h, _bits(i * (8 // len(off)), 8 // len(off))) for i, (o, h) in enumerate(off)]
+    call += [(o, h, _bits(8 + i * (8 // len(on)), 8 // len(on))) for i, (o, h) in enumerate(on)]
+    calls.append(call)
+    return calls
+
+
+def _plan2(o):
+    off = [r for r in range(NCHIP - 1, 0, -1) if r != o]
+    last = [off.pop()] if len(off) > 8 else []
+    long4, short4 = off[:4], off[4:][::-1]
+    calls = [[(r, _bits(2 * i, 2)) for i, r in enumerate(long4)],
+             [(r, _bits(2 * i, 2)) for i, r in enumerate(short4)]]
+    if o > 0:
+        calls[0].append((o, 0xFF00))
+    if last:
+        calls.append([(last[0], 0x00FF)])
+    return calls
 
 
 def rank_program(g, core, T, topo):
-    chip, k_on_chip = topo.chip(core), core % 8
+    chip, on_chip = topo.chip(core), core % 8
     if chip >= NCHIP:
         return
-    pair, par = chip // 2, chip % 2
 
     def dst(c):
         rid, pid, _se = topo.addr(c)
         return DstId(rid=rid, pnc=pid)
 
-    e1 = 8 // S
+    def piece(bufB, bufA, o, h):
+        return bufB[o * NH + h] if o < SMALL else bufA[(o - SMALL) * NH + h]
 
-    if k_on_chip == RANK_CORE:
-        g.sync.dma_start(T.xs[:], T.x[:]).then_inc(T.sem.ld, 16)
-        if chip == 0:
-            g.scalar.dma_start(T.y[:], T.x[:]).then_inc(T.sem.st, 16)
-        g.wait_ge(T.sem.ld, 16)
-        tr = []
-        for s in range(S):
-            tr.append(RemoteDMATransfer(dst_ids=[dst(chip * 8 + HELP[s])], dma_engine_mask=_bits(8 + s * e1, e1),
-                                        remote_sem=T.sem.in1, src=T.xs[s], dst=T.own[:]))
-            if _needs_mate(chip ^ 1):
-                tr.append(RemoteDMATransfer(dst_ids=[dst((chip ^ 1) * 8 + HELP[s])], dma_engine_mask=_bits(s * e1, e1),
-                                            remote_sem=T.sem.in1, src=T.xs[s], dst=T.mate[:]))
-        g.remote_dma_fused(tr, local_sem=T.sem.sent)
-        if chip > 0:
-            g.sync.wait_ge(T.sem.in2, S * (8 if chip == 1 else 16))
-            g.sync.dma_start(T.y[:], T.res[:]).then_inc(T.sem.st, 16)
-        g.wait_ge(T.sem.sent, e1 * len(tr))
-        g.wait_ge(T.sem.st, 16)
+    if on_chip == RANK_CORE:
+        j = chip
+        g.sync.dma_start(T.xsA[:], T.x[ROWS_B:128, :]).then_inc(T.sem.ld, 16)
+        g.scalar.dma_start(T.xsB[:], T.x[0:ROWS_B, :]).then_inc(T.sem.ld, 16)
+        g.wait_ge(T.sem.ld, 32)
+        sent = 0
+        for call in _plan1(j):
+            tr = []
+            for o, h, m in call:
+                gbuf = T.gB if o < SMALL else T.gA
+                tr.append(RemoteDMATransfer(dst_ids=[dst(o * 8 + HELP[h])], dma_engine_mask=m, remote_sem=T.sem.in1,
+                                            src=piece(T.xsB, T.xsA, o, h), dst=gbuf[j]))
+                sent += _pop(m)
+            g.remote_dma_fused(tr, local_sem=T.sem.sent)
+        if j == 0:
+            g.sync.dma_start(T.y[ROWS_B:128, :], T.x[ROWS_B:128, :]).then_inc(T.sem.st, 16)
+            g.scalar.dma_start(T.y[0:ROWS_B, :], T.x[0:ROWS_B, :]).then_inc(T.sem.st, 16)
+        else:
+            landed = NH * sum(_pop(m) for o in range(NCHIP) for call in _plan2(o) for r, m in call if r == j)
+            g.sync.wait_ge(T.sem.in2, landed)
+            g.sync.dma_start(T.y[ROWS_B:128, :], T.resA[:]).then_inc(T.sem.st, 16)
+            g.scalar.wait_ge(T.sem.in2, landed)
+            g.scalar.dma_start(T.y[0:ROWS_B, :], T.resB[:]).then_inc(T.sem.st, 16)
+        g.wait_ge(T.sem.sent, sent)
+        g.wait_ge(T.sem.st, 32)
         return
 
-    if k_on_chip not in HELP:
+    if on_chip not in HELP:
         return
-    s = HELP.index(k_on_chip)
-    rank_core = chip * 8 + RANK_CORE
+    o, h = chip, HELP.index(on_chip)
+    gbuf = T.gB if o < SMALL else T.gA
+    g.wait_ge(T.sem.in1, sum(_pop(m) for j in range(NCHIP) for call in _plan1(j)
+                             for oo, hh, m in call if (oo, hh) == (o, h)))
     sent = 0
-    g.wait_ge(T.sem.in1, e1 * (2 if _needs_mate(chip) else 1))
-
-    if pair < NPAIR - 1:
-        ids = [dst((2 * q + par) * 8 + k_on_chip) for q in range(pair + 1, NPAIR)]
-        outs = [T.pre[pair] for _q in range(pair + 1, NPAIR)]
-        if chip == 1:
-            ids.append(dst(rank_core))
-            outs.append(T.res[s])
-        g.remote_dma_fused([RemoteDMATransfer(dst_ids=ids, dma_engine_mask=0x00FF, remote_sem=T.sem.in2,
-                                              srcs=[T.own[:], T.mate[:]], dsts=outs, alu_op=MAX)],
-                           local_sem=T.sem.sent)
-        sent += 8
-
-    if pair > 0:
-        g.wait_ge(T.sem.in2, 8 * pair)
-        srcs = [T.pre[j] for j in range(pair)] + [T.own[:]] + ([T.mate[:]] if par else [])
-        g.remote_dma_fused([RemoteDMATransfer(dst_ids=[dst(rank_core)], dma_engine_mask=0xFFFF, remote_sem=T.sem.in2,
-                                              srcs=srcs, dsts=[T.res[s]], alu_op=MAX)],
-                           local_sem=T.sem.sent)
-        sent += 16
-
+    for call in _plan2(o):
+        tr = []
+        for r, m in call:
+            tr.append(RemoteDMATransfer(dst_ids=[dst(r * 8 + RANK_CORE)], dma_engine_mask=m, remote_sem=T.sem.in2,
+                                        srcs=[gbuf[j] for j in range(r + 1)], dsts=[piece(T.resB, T.resA, o, h)],
+                                        alu_op=MAX))
+            sent += _pop(m)
+        g.remote_dma_fused(tr, local_sem=T.sem.sent)
     g.wait_ge(T.sem.sent, sent)

from concourse.bass import DstId, RemoteDMATransfer

NCHIP = 10
RANK_CORE = 7
HELP = [2, 3]
NH = len(HELP)
SMALL = 2
WB, WA = 24 // NH, 26 // NH
ROWS_B = SMALL * 12
MAX = 2

SCRATCH = {
    "xsB": ("dram", [SMALL * NH, 128, WB], "float32"),
    "xsA": ("dram", [(NCHIP - SMALL) * NH, 128, WA], "float32"),
    "resB": ("dram", [SMALL * NH, 128, WB], "float32"),
    "resA": ("dram", [(NCHIP - SMALL) * NH, 128, WA], "float32"),
    "gB": ("dram", [NCHIP, 128, WB], "float32"),
    "gA": ("dram", [NCHIP, 128, WA], "float32"),
}
SEMAPHORES = ["ld", "st", "in1", "in2", "sent"]


def _bits(lo, n):
    return ((1 << n) - 1) << lo


def _pop(m):
    return bin(m).count("1")


def _plan1(j):
    calls = []
    for h in range(NH):
        call, e = [], 0
        for o in range(SMALL, NCHIP):
            if o == j:
                call.append((o, h, 0xFF00))
            else:
                call.append((o, h, _bits(e, 1)))
                e += 1
        calls.append(call)
    units = [(o, h) for o in range(SMALL) for h in range(NH)]
    off = [u for u in units if u[0] != j]
    on = [u for u in units if u[0] == j]
    call = [(o, h, _bits(i * (8 // len(off)), 8 // len(off))) for i, (o, h) in enumerate(off)]
    call += [(o, h, _bits(8 + i * (8 // len(on)), 8 // len(on))) for i, (o, h) in enumerate(on)]
    calls.append(call)
    return calls


def _plan2(o):
    off = [r for r in range(NCHIP - 1, 0, -1) if r != o]
    last = [off.pop()] if len(off) > 8 else []
    long4, short4 = off[:4], off[4:][::-1]
    calls = [[(r, _bits(2 * i, 2)) for i, r in enumerate(long4)],
             [(r, _bits(2 * i, 2)) for i, r in enumerate(short4)]]
    if o > 0:
        calls[0].append((o, 0xFF00))
    if last:
        calls.append([(last[0], 0x00FF)])
    return calls


def rank_program(g, core, T, topo):
    chip, on_chip = topo.chip(core), core % 8
    if chip >= NCHIP:
        return

    def dst(c):
        rid, pid, _se = topo.addr(c)
        return DstId(rid=rid, pnc=pid)

    def piece(bufB, bufA, o, h):
        return bufB[o * NH + h] if o < SMALL else bufA[(o - SMALL) * NH + h]

    if on_chip == RANK_CORE:
        j = chip
        g.sync.dma_start(T.xsA[:], T.x[ROWS_B:128, :]).then_inc(T.sem.ld, 16)
        g.scalar.dma_start(T.xsB[:], T.x[0:ROWS_B, :]).then_inc(T.sem.ld, 16)
        g.wait_ge(T.sem.ld, 32)
        sent = 0
        for call in _plan1(j):
            tr = []
            for o, h, m in call:
                gbuf = T.gB if o < SMALL else T.gA
                tr.append(RemoteDMATransfer(dst_ids=[dst(o * 8 + HELP[h])], dma_engine_mask=m, remote_sem=T.sem.in1,
                                            src=piece(T.xsB, T.xsA, o, h), dst=gbuf[j]))
                sent += _pop(m)
            g.remote_dma_fused(tr, local_sem=T.sem.sent)
        if j == 0:
            g.sync.dma_start(T.y[ROWS_B:128, :], T.x[ROWS_B:128, :]).then_inc(T.sem.st, 16)
            g.scalar.dma_start(T.y[0:ROWS_B, :], T.x[0:ROWS_B, :]).then_inc(T.sem.st, 16)
        else:
            landed = NH * sum(_pop(m) for o in range(NCHIP) for call in _plan2(o) for r, m in call if r == j)
            g.sync.wait_ge(T.sem.in2, landed)
            g.sync.dma_start(T.y[ROWS_B:128, :], T.resA[:]).then_inc(T.sem.st, 16)
            g.scalar.wait_ge(T.sem.in2, landed)
            g.scalar.dma_start(T.y[0:ROWS_B, :], T.resB[:]).then_inc(T.sem.st, 16)
        g.wait_ge(T.sem.sent, sent)
        g.wait_ge(T.sem.st, 32)
        return

    if on_chip not in HELP:
        return
    o, h = chip, HELP.index(on_chip)
    gbuf = T.gB if o < SMALL else T.gA
    g.wait_ge(T.sem.in1, sum(_pop(m) for j in range(NCHIP) for call in _plan1(j)
                             for oo, hh, m in call if (oo, hh) == (o, h)))
    sent = 0
    for call in _plan2(o):
        tr = []
        for r, m in call:
            tr.append(RemoteDMATransfer(dst_ids=[dst(r * 8 + RANK_CORE)], dma_engine_mask=m, remote_sem=T.sem.in2,
                                        srcs=[gbuf[j] for j in range(r + 1)], dsts=[piece(T.resB, T.resA, o, h)],
                                        alu_op=MAX))
            sent += _pop(m)
        g.remote_dma_fused(tr, local_sem=T.sem.sent)
    g.wait_ge(T.sem.sent, sent)
